import numpy as np
import ml_dtypes


def mxq(x, axis, fmt="e4m3"):
    dtype, down = {"e4m3": (ml_dtypes.float8_e4m3fn, 7), "e5m2": (ml_dtypes.float8_e5m2, 14)}[fmt]
    v = np.moveaxis(np.asarray(x, np.float32).astype(ml_dtypes.bfloat16).astype(np.float64), axis, -1)
    blocks = v.reshape(v.shape[:-1] + (-1, 32))
    amax = np.abs(blocks).max(-1, keepdims=True)
    byte = np.maximum(np.where(amax > 0, np.frexp(amax)[1] - 1 + 127, 0) - down, 1)
    scale = np.exp2(byte - 127.0)
    codes = (blocks / scale).astype(np.float32).astype(dtype).astype(np.float64)
    return np.moveaxis((codes * scale).reshape(v.shape), -1, axis)


WIDE = False


def mx_kscale(k):
    if not WIDE:
        return np.ones(k)
    levels = np.array([10, -10, 5, -5, 0])
    if k % 512:
        return np.exp2(np.random.permutation(np.resize(levels, k // 32))).repeat(32)
    a = np.empty((k // 512, 16))
    for p in range(k // 512):
        a[p, :8] = np.random.permutation(np.resize(levels, 8))
        for g in range(8):
            far = levels[np.abs(levels - a[p, g]) >= 10]
            a[p, g + 8] = far[np.random.randint(len(far))]
    return np.exp2(a.ravel()).repeat(32)


BF16 = ml_dtypes.bfloat16


def bf(x):
    return np.asarray(x, np.float32).astype(BF16)


def f64(x):
    return np.asarray(x).astype(np.float64)

def planes(Y):
    n, m = Y.shape
    b = f64(bf(Y)).reshape(n // 32, 32, m)
    amax = np.abs(b).max(1)
    byte = np.clip(np.where(amax > 0, np.frexp(amax)[1] - 1 + 127 - 7, 1), 1, 254)
    codes = (b * np.exp2(127.0 - byte)[:, None, :]).reshape(n, m).astype(np.float32).astype(ml_dtypes.float8_e4m3fn).view(np.uint8)
    words = codes.reshape(n // 512, 128, 4, m).transpose(0, 1, 3, 2)
    return np.ascontiguousarray(words), np.ascontiguousarray(byte.astype(np.uint8).reshape(n // 512, 16, m))


B, S, D, H, E = 2, 512, 1024, 2, 512


def project_heads(xq, wq):
    return xq[:, None] @ wq[None]


def softmax_last(z):
    shifted = z - np.max(z, axis=-1, keepdims=True)
    e = np.exp(shifted)
    return e / np.sum(e, axis=-1, keepdims=True)


def setup_inputs():
    s, t = mx_kscale(D), mx_kscale(E)
    return {
        "x": bf(np.random.standard_normal((B, S, D)) * s),
        "wq": bf(np.random.standard_normal((H, D, E)) / np.sqrt(D) / s[:, None] * t),
        "wk": bf(np.random.standard_normal((H, D, E)) / np.sqrt(D) / s[:, None] / t),
        "lk": bf(1.0 + 0.1 * np.random.standard_normal((B, H, E))),
    }


def core(x, wq, wk, lk):
    xq = mxq(f64(x), 2, "e4m3")
    q = project_heads(xq, mxq(f64(wq), 1, "e4m3"))
    k = project_heads(xq, mxq(f64(wk), 1, "e4m3"))
    ks = k * f64(lk)[:, :, None, :]
    z = (mxq(q, 3, "e4m3") @ mxq(ks, 3, "e4m3").transpose(0, 1, 3, 2)) / np.sqrt(E)
    return S * softmax_last(z)


def reference(x, wq, wk, lk):
    R_out = core(x, wq, wk, lk)
    words, scales = planes(np.moveaxis(R_out, 2, 0).reshape(512, -1))
    return R_out, words, scales

@@ -1,0 +1,320 @@
+import math
+from contextlib import ExitStack
+
+import concourse.mybir as mybir
+from concourse.masks import make_identity
+
+B, S, D, H, E = 2, 512, 1024, 2, 512
+FLOPS = 2 * B * H * (2 * S * D * E + S * S * E)
+
+F32 = mybir.dt.float32
+BF16 = mybir.dt.bfloat16
+U32 = mybir.dt.uint32
+I32 = mybir.dt.int32
+U8 = mybir.dt.uint8
+FP8X4 = mybir.dt.float8_e4m3fn_x4
+ALU = mybir.AluOpType
+ACT = mybir.ActivationFunctionType
+AX = mybir.AxisListType
+
+P = 128
+PACK = 4
+G = D // 512
+NC = S // P
+SCALE = 1.0 / math.sqrt(E)
+UNITS = [(0, 0), (1, 0), (0, 1), (1, 1)]
+BANKS = {'aux': 2, 'proj': 3, 'z': 3}
+LOADS = [('x', 0, 1), ('x', 1, 0), ('k', 0, 1), ('k', 0, 0), ('x', 0, 0), ('x', 0, 3), ('x', 0, 2), ('x', 1, 2), ('q', 0, 0), ('q', 0, 1), ('x', 1, 3), ('lk',), ('q', 1, 0), ('x', 1, 1), ('q', 1, 1), ('k', 1, 0), ('k', 1, 1)]
+WAY = {('k', 0, 0, 0): 'V', ('k', 0, 0, 1): 'S', ('k', 0, 1, 0): 'V', ('k', 0, 1, 1): 'S', ('k', 1, 0, 0): 'TS', ('k', 1, 0, 1): 'V', ('k', 1, 1, 0): 'V', ('k', 1, 1, 1): 'TS', ('q', 0, 0, 0): 'S', ('q', 0, 0, 1): 'V', ('q', 0, 1, 0): 'TS', ('q', 0, 1, 1): 'S', ('q', 1, 0, 0): 'S', ('q', 1, 0, 1): 'S', ('q', 1, 1, 0): 'S', ('q', 1, 1, 1): 'S'}
+SC = ['GGGG', 'GGGG', 'VVVV', 'VVVV']
+PI = ['S', 'S', 'VS', 'VS']
+XC = ['V', 'V', 'S', 'S', 'S', 'S', 'V', 'S']
+ORDER = (
+    "xt.0.1 xt.1.0 xc.0.1 xc.1.0 xq.0.1 wi.k.0.1.0 wi.k.0.1.1 xq.1.0 wi.k.0.0.0 wi.k.0.0.1 xt.0.0 wq.k.0.1 xt.0.3 "
+    "xc.0.0 xc.0.3 wq.k.0.0 xt.0.2 xq.0.0 xt.1.2 xc.0.2 xq.0.3 p.k.0.1 xc.1.2 wi.q.0.0.0 xq.0.2 p.k.0.3 wi.q.0.0.1 "
+    "p.k.0.2 wi.q.0.1.1 xq.1.2 wq.q.0.0 wt.q.0.1.0 xt.1.3 ev.k.0.2 wi.q.0.1.0 ev.k.0.1 p.k.0.0 xc.1.3 wq.q.0.1 "
+    "wi.q.1.0.1 p.k.1.2 ev.k.0.0 xt.1.1 ev.k.0.3 wi.q.1.0.0 p.q.0.0 ev.k.1.2 qz.k.0 p.q.0.1 ev.q.0.0 wi.k.1.0.1 "
+    "p.q.0.3 ev.q.0.1 xq.1.3 p.q.0.2 wq.q.1.0 ev.q.0.3 p.k.1.3 wi.k.1.1.0 ev.q.0.2 p.q.1.2 xc.1.1 ev.k.1.3 p.k.1.0 "
+    "wi.q.1.1.1 qz.q.0 p.q.1.3 xq.1.1 ev.k.1.0 z.0.2 ev.q.1.2 z.0.3 mx.0.2 z.0.1 ev.q.1.3 p.k.1.1 mx.0.1 wi.q.1.1.0 "
+    "wt.k.1.0.0 mx.0.3 p.q.1.0 ev.k.1.1 wi.k.1.0.0 nb.0.1 wq.q.1.1 wt.k.1.1.1 ex.0.3 qz.k.1 p.q.1.1 ex.0.2 wq.k.1.0 "
+    "z.0.0 wi.k.1.1.1 p.q.2.0 mx.0.0 ev.q.1.1 wq.k.1.1 ev.q.1.0 p.q.2.2 nb.0.0 ex.0.0 qz.q.1 p.k.2.3 ex.0.1 z.1.0 "
+    "ev.k.2.3 z.1.2 ev.q.2.2 z.1.1 inv.0 p.q.2.3 mx.1.2 sc.0.2 ev.q.2.0 mx.1.1 p.q.2.1 sc.0.0 ev.q.2.3 mx.1.0 "
+    "p.k.2.1 sc.0.1 ev.q.2.1 p.k.2.2 nb.1.0 sc.0.3 ev.k.2.1 ex.1.1 p.k.2.0 qz.q.2 pi.0.0 z.1.3 ev.k.2.2 p.k.3.0 "
+    "mx.1.3 p.q.3.2 ev.k.2.0 nb.1.1 ev.k.3.0 p.q.3.1 ex.1.3 pq.0.0 p.k.3.2 ex.1.0 qz.k.2 ex.1.2 ev.k.3.2 z.2.0 "
+    "z.2.2 ev.q.3.1 inv.1 z.2.3 mx.2.0 sc.1.1 p.q.3.0 ev.q.3.2 mx.2.2 sc.1.0 p.q.3.3 ev.q.3.0 mx.2.3 sc.1.2 p.k.3.3 "
+    "ev.q.3.3 nb.2.1 sc.1.3 p.k.3.1 ex.2.3 ev.k.3.3 pi.1.0 qz.q.3 z.2.1 mx.2.1 rc.2.3 ev.k.3.1 sc.2.3 nb.2.0 qz.k.3 "
+    "ex.2.1 pq.1.0 ex.2.0 z.3.3 rc.2.1 sc.2.1 ex.2.2 mx.3.3 z.3.0 mx.3.0 z.3.1 mx.3.1 rc.2.0 rc.2.2 nb.3.0 sc.2.0 "
+    "ex.3.0 sc.2.2 pi.2.1 pi.2.0 z.3.2 mx.3.2 pq.2.0 ex.3.1 nb.3.1 pq.2.1 ex.3.3 rc.3.0 rc.3.1 sc.3.0 sc.3.1 ex.3.2 "
+    "rc.3.3 sc.3.3 rc.3.2 sc.3.2 pi.3.1 pi.3.0 pq.3.0 pq.3.1 "
+).split()
+
+
+def tile_ia3mixedtaskkeyattentionlift_x1_kernel(tc, x, wq, wk, lk, out, words, scales):
+    nc = tc.nc
+    words32 = words.rearrange("g p m t -> (g p) (m t)").bitcast(I32)
+    scales32 = scales.rearrange("g q m -> (g q) m").bitcast(I32)
+
+    with ExitStack() as ctx:
+        keep = ctx.enter_context(tc.tile_pool(name="keep", bufs=1))
+        load = ctx.enter_context(tc.tile_pool(name="load", bufs=8))
+        work = ctx.enter_context(tc.tile_pool(name="work", bufs=2))
+        psum = ctx.enter_context(tc.psum_pool(name="psum", bufs=2))
+        ctx.enter_context(tc.manual_schedule())
+
+        x_raw = {}
+        w_raw = {}
+        w_in = {"q": wq, "k": wk}
+
+        def load_x(b, c):
+            t = load.tile([P, D], BF16, name="x_rows", align_bytes=64)
+            nc.sync.dma_start(out=t[:], in_=x[b, c * P : (c + 1) * P, :])
+            x_raw[b, c] = t
+
+        def load_w(n, h, g):
+            t = load.tile([P, PACK, E], BF16, name="w_rows", align_bytes=64)
+            nc.sync.dma_start(out=t[:], in_=w_in[n][h, g * 512 : (g + 1) * 512, :].rearrange("(p j) w -> p j w", j=PACK))
+            w_raw[n, h, g] = t
+
+        lk_t = keep.tile([P, B * H, PACK], BF16)
+        for item in LOADS:
+            if item[0] == "lk":
+                nc.sync.dma_start(out=lk_t[:], in_=lk.rearrange("b h (p t) -> p (b h) t", t=PACK))
+            elif item[0] == "x":
+                load_x(item[1], item[2])
+            else:
+                load_w(item[0], item[1], item[2])
+
+        ident = keep.tile([P, P], F32, align_bytes=64)
+        make_identity(nc, ident[:])
+        ident_bf = keep.tile([P, P], BF16, align_bytes=64)
+        nc.gpsimd.tensor_copy(out=ident_bf[:], in_=ident[:])
+        warm = keep.tile([P, 1], F32)
+        nc.vector.memset(warm[:], 0.0)
+        warm_out = keep.tile([P, 1], F32)
+        nc.scalar.activation(out=warm_out[:], in_=warm[:], func=ACT.Exp)
+
+        x_q = {}
+        w_q = {}
+        x_bank = {}
+        x_mid = {}
+        w_mid = {}
+        w_bank = {}
+
+        def x_turn(b, c):
+            pairs = x_raw[b, c][:].bitcast(F32)
+            bank = psum.tile([P, G * 2, P], F32, name="aux", bufs=BANKS["aux"])
+            for g in range(G):
+                for u in range(2):
+                    nc.tensor.transpose(bank[:, 2 * g + u, :], pairs[:, 256 * g + u : 256 * (g + 1) : 2], ident[:])
+            x_bank[b, c] = bank
+
+        def x_copy(b, c):
+            grouped = work.tile([P, G, P, PACK], BF16, name="x_grouped", bufs=8, align_bytes=64)
+            (nc.scalar.copy if XC[4 * b + c] == "S" else nc.vector.tensor_copy)(
+                out=grouped[:].bitcast(F32),
+                in_=x_bank[b, c][:].rearrange("p (g u) r -> p g r u", u=2),
+            )
+            x_mid[b, c] = grouped
+
+        def x_quant(b, c):
+            codes = keep.tile([P, G, P], U32, name=f"x_codes_{b}{c}", align_bytes=64)
+            scl = keep.tile([P, G, P], U8, name=f"x_scales_{b}{c}", align_bytes=64)
+            nc.vector.quantize_mx(
+                out=codes[:].rearrange("p g r -> p (g r)").bitcast(FP8X4),
+                scales=scl[:].rearrange("p g r -> p (g r)"),
+                in_=x_mid[b, c][:].rearrange("p g r j -> p (g r j)"),
+            )
+            x_q[b, c] = (codes, scl)
+
+        def w_target(n, h, g):
+            if (n, h, g) not in w_mid:
+                w_mid[n, h, g] = work.tile([P, PACK, P * PACK], BF16, name="w_mid", bufs=6, align_bytes=64)
+            return w_mid[n, h, g]
+
+        def w_source(n, h, g):
+            return w_raw[n, h, g][:].rearrange("p j (m t) -> p t m j", t=PACK)
+
+        def w_turn(n, h, g, half):
+            src = w_source(n, h, g)
+            bank = psum.tile([P, 2, P * PACK], BF16, name="aux", bufs=BANKS["aux"])
+            for i in range(2):
+                nc.tensor.matmul(
+                    bank[:, i, :].rearrange("p (m j) -> p m j", j=PACK), lhsT=ident_bf[:], rhs=src[:, 2 * half + i], start=True, stop=True
+                )
+            w_bank[n, h, g, half] = bank
+
+        def w_interleave(n, h, g, half):
+            how = WAY[n, h, g, half]
+            dst = w_target(n, h, g)[:, 2 * half : 2 * half + 2, :]
+            if how in ("TS", "TV"):
+                (nc.scalar.copy if how == "TS" else nc.vector.tensor_copy)(out=dst, in_=w_bank[n, h, g, half][:])
+            else:
+                (nc.scalar.copy if how == "S" else nc.vector.tensor_copy)(
+                    out=dst.rearrange("p t (m j) -> p t m j", j=PACK), in_=w_source(n, h, g)[:, 2 * half : 2 * half + 2]
+                )
+
+        def w_quant(n, h, g):
+            codes = keep.tile([P, E], U32, name=f"w_codes_{n}{h}{g}", align_bytes=64)
+            scl = keep.tile([P, E], U8, name=f"w_scales_{n}{h}{g}", align_bytes=64)
+            nc.vector.quantize_mx(
+                out=codes[:].bitcast(FP8X4), scales=scl[:], in_=w_mid[n, h, g][:].rearrange("p t c -> p (t c)")
+            )
+            w_q[n, h, g] = (codes, scl)
+
+        st = {}
+
+        def project(n, u, c):
+            b, h = UNITS[u]
+            bank = psum.tile([P, PACK, P], F32, name="proj", bufs=BANKS["proj"])
+            x_codes, x_scl = x_q[b, c]
+            for t in range(PACK):
+                for g in range(G):
+                    w_codes, w_scl = w_q[n, h, g]
+                    nc.tensor.matmul_mx(
+                        out=bank[:, t, :],
+                        lhsT=w_codes[:, t * P : (t + 1) * P].bitcast(FP8X4),
+                        lhsT_scale=w_scl[:, t * P : (t + 1) * P],
+                        rhs=x_codes[:, g, :].bitcast(FP8X4),
+                        rhs_scale=x_scl[:, g, :],
+                        start=(g == 0),
+                        stop=(g == G - 1),
+                    )
+            st[n, u, c] = bank
+
+        def open_unit(u):
+            st["qg", u] = work.tile([P, PACK, P, PACK], BF16, name="q_grouped", bufs=3, align_bytes=64)
+            st["kg", u] = work.tile([P, S, PACK], BF16, name="k_grouped", bufs=3, align_bytes=64)
+
+        def q_out(u, c):
+            nc.scalar.copy(
+                out=st["qg", u][:, :, 32 * c : 32 * (c + 1), :],
+                in_=st["q", u, c][:].rearrange("p j (m t) -> p t m j", t=PACK),
+            )
+
+        def k_out(u, c):
+            b, h = UNITS[u]
+            nc.vector.tensor_mul(
+                out=st["kg", u][:, c * P : (c + 1) * P, :],
+                in0=st["k", u, c][:].rearrange("p j r -> p r j"),
+                in1=lk_t[:, b * H + h, :].unsqueeze(1).to_broadcast([P, P, PACK]),
+            )
+
+        def quantise(grouped, name):
+            codes = work.tile([P, S], U32, name=name + "_codes", bufs=4, align_bytes=64)
+            scl = work.tile([P, S], U8, name=name + "_scales", bufs=4, align_bytes=64)
+            nc.vector.quantize_mx(out=codes[:].bitcast(FP8X4), scales=scl[:], in_=grouped)
+            return codes, scl
+
+        def q_quant(u):
+            st["Q", u] = quantise(st["qg", u][:].rearrange("p t m j -> p (t m j)"), "q")
+
+        def k_quant(u):
+            st["K", u] = quantise(st["kg", u][:].rearrange("p r j -> p (r j)"), "k")
+
+        def open_scores(u):
+            for n in ("neg", "bias", "total", "inv"):
+                st[n, u] = work.tile([P, PACK], F32, name=n, bufs=4)
+            st["e", u] = work.tile([P, PACK, S], F32, name="e", bufs=3, align_bytes=64)
+            st["o", u] = work.tile([P, PACK, S], F32, name="o", bufs=3, align_bytes=64)
+
+        def score(u, t):
+            if ("e", u) not in st:
+                open_scores(u)
+            q_codes, q_scl = st["Q", u]
+            k_codes, k_scl = st["K", u]
+            z = psum.tile([P, S], F32, name="z", bufs=BANKS["z"])
+            nc.tensor.matmul_mx(
+                out=z[:],
+                lhsT=q_codes[:, t * P : (t + 1) * P].bitcast(FP8X4),
+                lhsT_scale=q_scl[:, t * P : (t + 1) * P],
+                rhs=k_codes[:].bitcast(FP8X4),
+                rhs_scale=k_scl[:],
+                start=True,
+                stop=True,
+            )
+            st["z", u, t] = z
+
+        def row_max(u, t):
+            nc.vector.tensor_reduce(out=st["neg", u][:, t : t + 1], in_=st["z", u, t][:], axis=AX.X, op=ALU.max, negate=True)
+
+        def row_bias(u, pair):
+            cols = slice(2 * pair, 2 * pair + 2)
+            nc.vector.tensor_scalar_mul(st["bias", u][:, cols], st["neg", u][:, cols], SCALE)
+
+        def row_exp(u, t):
+            nc.scalar.activation(
+                out=st["e", u][:, t, :], in_=st["z", u, t][:], func=ACT.Exp, bias=st["bias", u][:, t : t + 1], scale=SCALE,
+                accum_out=st["total", u][:, t : t + 1],
+            )
+
+        def inverse(u):
+            if "S" in SC[u]:
+                nc.vector.tensor_scalar_mul(st["inv", u][:], st["total", u][:], 1.0 / S)
+                nc.vector.reciprocal(st["inv", u][:], st["inv", u][:])
+            else:
+                nc.vector.reciprocal(st["inv", u][:], st["total", u][:])
+
+        def row_inverse(u, t):
+            nc.vector.reciprocal(st["inv", u][:, t : t + 1], st["total", u][:, t : t + 1])
+
+        left = {}
+
+        def row_scale(u, t):
+            b, h = UNITS[u]
+            o, e, inv = st["o", u][:, t, :], st["e", u][:, t, :], st["inv", u][:, t : t + 1]
+            if SC[u][t] == "S":
+                nc.scalar.activation(out=o, in_=e, func=ACT.Copy, scale=inv)
+            else:
+                eng = nc.gpsimd if SC[u][t] == "G" else nc.vector
+                eng.tensor_scalar(out=o, in0=e, scalar1=inv, scalar2=float(S), op0=ALU.mult, op1=ALU.mult)
+            pair = t // 2
+            left[u, pair] = left.get((u, pair), 0) + 1
+            if left[u, pair] == 2:
+                rows = slice(2 * pair, 2 * pair + 2)
+                nc.sync.dma_start(out=out[b, h].rearrange("(p t) k -> p t k", t=PACK)[:, rows], in_=st["o", u][:, rows])
+
+        def p_group(u, i):
+            parts = len(PI[u])
+            n = S // parts
+            cols = slice(i * n, i * n + n)
+            grouped = work.tile([P, n, PACK], BF16, name=f"p_grouped{parts}", bufs=3, align_bytes=64)
+            st["pg", u, i] = grouped
+            src = st["o", u][:, :, cols].rearrange("p t k -> p k t")
+            (nc.vector.tensor_copy if PI[u][i] == "V" else nc.scalar.copy)(out=grouped[:], in_=src)
+
+        def p_quant(u, i):
+            b, h = UNITS[u]
+            parts = len(PI[u])
+            n = S // parts
+            if ("pc", u) not in st:
+                st["pc", u] = work.tile([P, S], U32, name="p_codes", bufs=3, align_bytes=64)
+                st["ps", u] = work.tile([P, S], U8, name="p_scales", bufs=3, align_bytes=64)
+            codes, scl = st["pc", u], st["ps", u]
+            cols = slice(i * n, i * n + n)
+            nc.vector.quantize_mx(
+                out=codes[:, cols].bitcast(FP8X4), scales=scl[:, cols], in_=st["pg", u, i][:].rearrange("p k t -> p (k t)")
+            )
+            left["pq", u] = left.get(("pq", u), 0) + 1
+            if left["pq", u] == parts:
+                col = (b * H + h) * S
+                nc.sync.dma_start(out=words32[:, col : col + S], in_=codes[:].bitcast(I32))
+                for quad in range(4):
+                    nc.sync.dma_start(
+                        out=scales32[4 * quad : 4 * quad + 4, col // 4 : (col + S) // 4],
+                        in_=scl[32 * quad : 32 * quad + 4, :].bitcast(I32),
+                    )
+
+        def evacuate(n, u, c):
+            if ("qg", u) not in st:
+                open_unit(u)
+            (q_out if n == "q" else k_out)(u, c)
+
+        steps = {
+            "xt": x_turn, "xc": x_copy, "xq": x_quant, "wt": w_turn, "wi": w_interleave, "wq": w_quant,
+            "p": project, "ev": evacuate, "qz": lambda n, u: (q_quant if n == "q" else k_quant)(u),
+            "z": score, "mx": row_max, "nb": row_bias, "ex": row_exp, "inv": inverse, "rc": row_inverse,
+            "sc": row_scale, "pi": p_group, "pq": p_quant,
+        }
+        for name in ORDER:
+            kind, *idx = name.split(".")
+            steps[kind](*[a if a in ("q", "k") else int(a) for a in idx])

@@ -24,28 +24,28 @@ NC = S // P
 SCALE = 1.0 / math.sqrt(E)
 UNITS = [(0, 0), (1, 0), (0, 1), (1, 1)]
 BANKS = {'aux': 2, 'proj': 3, 'z': 3}
-LOADS = [('x', 0, 1), ('x', 1, 0), ('k', 0, 1), ('k', 0, 0), ('x', 0, 0), ('x', 0, 3), ('x', 0, 2), ('x', 1, 2), ('q', 0, 0), ('q', 0, 1), ('x', 1, 3), ('lk',), ('q', 1, 0), ('x', 1, 1), ('q', 1, 1), ('k', 1, 0), ('k', 1, 1)]
-WAY = {('k', 0, 0, 0): 'V', ('k', 0, 0, 1): 'S', ('k', 0, 1, 0): 'V', ('k', 0, 1, 1): 'S', ('k', 1, 0, 0): 'TS', ('k', 1, 0, 1): 'V', ('k', 1, 1, 0): 'V', ('k', 1, 1, 1): 'TS', ('q', 0, 0, 0): 'S', ('q', 0, 0, 1): 'V', ('q', 0, 1, 0): 'TS', ('q', 0, 1, 1): 'S', ('q', 1, 0, 0): 'S', ('q', 1, 0, 1): 'S', ('q', 1, 1, 0): 'S', ('q', 1, 1, 1): 'S'}
-SC = ['GGGG', 'GGGG', 'VVVV', 'VVVV']
-PI = ['S', 'S', 'VS', 'VS']
-XC = ['V', 'V', 'S', 'S', 'S', 'S', 'V', 'S']
+LOADS = [('x', 1, 2), ('k', 0, 1), ('k', 0, 0), ('x', 0, 1), ('x', 0, 0), ('q', 0, 1), ('lk',), ('x', 0, 2), ('q', 0, 0), ('x', 1, 3), ('q', 1, 0), ('x', 0, 3), ('q', 1, 1), ('k', 1, 0), ('x', 1, 0), ('x', 1, 1), ('k', 1, 1)]
+WAY = {('k', 0, 0, 0): 'S', ('k', 0, 0, 1): 'V', ('k', 0, 1, 0): 'S', ('k', 0, 1, 1): 'V', ('k', 1, 0, 0): 'S', ('k', 1, 0, 1): 'S', ('k', 1, 1, 0): 'S', ('k', 1, 1, 1): 'V', ('q', 0, 0, 0): 'V', ('q', 0, 0, 1): 'S', ('q', 0, 1, 0): 'S', ('q', 0, 1, 1): 'V', ('q', 1, 0, 0): 'V', ('q', 1, 0, 1): 'S', ('q', 1, 1, 0): 'V', ('q', 1, 1, 1): 'S'}
+SC = ['SSSS', 'SSSS', 'VVVV', 'VVVV']
+PI = ['S', 'VS', 'VS', 'VS']
+XC = ['S', 'S', 'S', 'V', 'V', 'S', 'V', 'S']
 ORDER = (
-    "xt.0.1 xt.1.0 xc.0.1 xc.1.0 xq.0.1 wi.k.0.1.0 wi.k.0.1.1 xq.1.0 wi.k.0.0.0 wi.k.0.0.1 xt.0.0 wq.k.0.1 xt.0.3 "
-    "xc.0.0 xc.0.3 wq.k.0.0 xt.0.2 xq.0.0 xt.1.2 xc.0.2 xq.0.3 p.k.0.1 xc.1.2 wi.q.0.0.0 xq.0.2 p.k.0.3 wi.q.0.0.1 "
-    "p.k.0.2 wi.q.0.1.1 xq.1.2 wq.q.0.0 wt.q.0.1.0 xt.1.3 ev.k.0.2 wi.q.0.1.0 ev.k.0.1 p.k.0.0 xc.1.3 wq.q.0.1 "
-    "wi.q.1.0.1 p.k.1.2 ev.k.0.0 xt.1.1 ev.k.0.3 wi.q.1.0.0 p.q.0.0 ev.k.1.2 qz.k.0 p.q.0.1 ev.q.0.0 wi.k.1.0.1 "
-    "p.q.0.3 ev.q.0.1 xq.1.3 p.q.0.2 wq.q.1.0 ev.q.0.3 p.k.1.3 wi.k.1.1.0 ev.q.0.2 p.q.1.2 xc.1.1 ev.k.1.3 p.k.1.0 "
-    "wi.q.1.1.1 qz.q.0 p.q.1.3 xq.1.1 ev.k.1.0 z.0.2 ev.q.1.2 z.0.3 mx.0.2 z.0.1 ev.q.1.3 p.k.1.1 mx.0.1 wi.q.1.1.0 "
-    "wt.k.1.0.0 mx.0.3 p.q.1.0 ev.k.1.1 wi.k.1.0.0 nb.0.1 wq.q.1.1 wt.k.1.1.1 ex.0.3 qz.k.1 p.q.1.1 ex.0.2 wq.k.1.0 "
-    "z.0.0 wi.k.1.1.1 p.q.2.0 mx.0.0 ev.q.1.1 wq.k.1.1 ev.q.1.0 p.q.2.2 nb.0.0 ex.0.0 qz.q.1 p.k.2.3 ex.0.1 z.1.0 "
-    "ev.k.2.3 z.1.2 ev.q.2.2 z.1.1 inv.0 p.q.2.3 mx.1.2 sc.0.2 ev.q.2.0 mx.1.1 p.q.2.1 sc.0.0 ev.q.2.3 mx.1.0 "
-    "p.k.2.1 sc.0.1 ev.q.2.1 p.k.2.2 nb.1.0 sc.0.3 ev.k.2.1 ex.1.1 p.k.2.0 qz.q.2 pi.0.0 z.1.3 ev.k.2.2 p.k.3.0 "
-    "mx.1.3 p.q.3.2 ev.k.2.0 nb.1.1 ev.k.3.0 p.q.3.1 ex.1.3 pq.0.0 p.k.3.2 ex.1.0 qz.k.2 ex.1.2 ev.k.3.2 z.2.0 "
-    "z.2.2 ev.q.3.1 inv.1 z.2.3 mx.2.0 sc.1.1 p.q.3.0 ev.q.3.2 mx.2.2 sc.1.0 p.q.3.3 ev.q.3.0 mx.2.3 sc.1.2 p.k.3.3 "
-    "ev.q.3.3 nb.2.1 sc.1.3 p.k.3.1 ex.2.3 ev.k.3.3 pi.1.0 qz.q.3 z.2.1 mx.2.1 rc.2.3 ev.k.3.1 sc.2.3 nb.2.0 qz.k.3 "
-    "ex.2.1 pq.1.0 ex.2.0 z.3.3 rc.2.1 sc.2.1 ex.2.2 mx.3.3 z.3.0 mx.3.0 z.3.1 mx.3.1 rc.2.0 rc.2.2 nb.3.0 sc.2.0 "
-    "ex.3.0 sc.2.2 pi.2.1 pi.2.0 z.3.2 mx.3.2 pq.2.0 ex.3.1 nb.3.1 pq.2.1 ex.3.3 rc.3.0 rc.3.1 sc.3.0 sc.3.1 ex.3.2 "
-    "rc.3.3 sc.3.3 rc.3.2 sc.3.2 pi.3.1 pi.3.0 pq.3.0 pq.3.1 "
+    "xt.1.2 xc.1.2 wi.k.0.1.0 wi.k.0.1.1 xq.1.2 wi.k.0.0.1 wi.k.0.0.0 xt.0.1 wq.k.0.1 xt.0.0 xc.0.1 wq.k.0.0 xc.0.0 "
+    "xq.0.1 lk p.k.1.2 wi.q.0.1.1 wi.q.0.1.0 p.k.0.1 xq.0.0 ev.k.1.2 p.k.0.0 wq.q.0.1 wi.q.0.0.1 xt.0.2 wi.q.0.0.0 "
+    "xt.1.3 ev.k.0.1 xc.0.2 wq.q.0.0 wi.q.1.0.1 xt.0.3 xq.0.2 ev.k.0.0 p.q.0.2 xc.1.3 xc.0.3 p.q.0.0 wi.q.1.1.1 "
+    "wi.q.1.1.0 p.k.0.2 xq.0.3 xq.1.3 ev.q.0.2 wq.q.1.1 xt.1.0 ev.q.0.0 ev.k.0.2 p.q.0.1 wi.k.1.0.0 wi.q.1.0.0 "
+    "p.k.0.3 xc.1.0 p.q.0.3 ev.q.0.1 ev.k.0.3 xt.1.1 wi.k.1.0.1 xq.1.0 qz.k.0 p.q.1.3 wq.q.1.0 ev.q.0.3 p.k.1.3 "
+    "wi.k.1.1.1 ev.q.1.3 p.q.1.2 xc.1.1 qz.q.0 p.q.1.0 ev.q.1.2 ev.k.1.3 z.0.1 ev.q.1.0 xq.1.1 z.0.2 mx.0.1 z.0.0 "
+    "wi.k.1.1.0 p.q.1.1 mx.0.0 p.k.1.1 mx.0.2 ev.q.1.1 p.k.1.0 nb.0.0 ev.k.1.1 ex.0.0 p.q.2.1 qz.q.1 ex.0.1 z.0.3 "
+    "ev.k.1.0 p.q.2.3 ev.q.2.1 mx.0.3 p.q.2.0 ev.q.2.3 qz.k.1 p.q.2.2 ev.q.2.0 nb.0.1 wq.k.1.1 z.1.3 ex.0.2 p.q.3.3 "
+    "wq.k.1.0 ex.0.3 mx.1.3 z.1.2 p.k.2.1 ev.q.2.2 inv.0 mx.1.2 z.1.0 sc.0.2 p.k.2.3 ev.k.2.1 ev.q.3.3 nb.1.1 "
+    "mx.1.0 p.k.2.0 ex.1.3 ev.k.2.3 p.k.2.2 ex.1.2 ev.k.2.0 z.1.1 sc.0.1 p.q.3.2 ev.k.2.2 sc.0.3 p.k.3.3 mx.1.1 "
+    "sc.0.0 qz.k.2 p.q.3.0 ev.q.3.2 nb.1.0 qz.q.2 ex.1.1 p.k.3.1 ev.k.3.3 ex.1.0 z.2.2 ev.k.3.1 z.2.0 ev.q.3.0 "
+    "p.k.3.2 mx.2.2 pi.0.0 z.2.1 mx.2.0 p.k.3.0 mx.2.1 p.q.3.1 inv.1 nb.2.0 ev.k.3.2 ev.k.3.0 ex.2.0 pq.0.0 "
+    "ev.q.3.1 z.2.3 qz.k.3 ex.2.1 mx.2.3 sc.1.2 rc.2.1 rc.2.0 nb.2.1 qz.q.3 ex.2.3 sc.2.1 z.3.1 ex.2.2 sc.2.0 z.3.3 "
+    "mx.3.1 sc.1.0 z.3.0 mx.3.3 sc.1.3 mx.3.0 sc.1.1 rc.2.3 rc.2.2 nb.3.0 sc.2.3 ex.3.0 sc.2.2 pi.1.0 ex.3.1 z.3.2 "
+    "mx.3.2 pi.2.1 pq.1.0 nb.3.1 rc.3.0 rc.3.1 pi.2.0 ex.3.3 pq.2.1 ex.3.2 pq.2.0 sc.3.1 pi.1.1 rc.3.3 rc.3.2 "
+    "sc.3.0 sc.3.2 sc.3.3 pi.3.1 pi.3.0 pq.1.1 pq.3.0 pq.3.1 "
 ).split()
 
 
@@ -75,10 +75,11 @@ def tile_ia3mixedtaskkeyattentionlift_x1_kernel(tc, x, wq, wk, lk, out, words, s
             nc.sync.dma_start(out=t[:], in_=w_in[n][h, g * 512 : (g + 1) * 512, :].rearrange("(p j) w -> p j w", j=PACK))
             w_raw[n, h, g] = t
 
-        lk_t = keep.tile([P, B * H, PACK], BF16)
+        lk_rows = keep.tile([P, E], BF16, align_bytes=64)
+        nc.gpsimd.memset(lk_rows[:], 0.0)
         for item in LOADS:
             if item[0] == "lk":
-                nc.sync.dma_start(out=lk_t[:], in_=lk.rearrange("b h (p t) -> p (b h) t", t=PACK))
+                nc.sync.dma_start(out=lk_rows[0 : B * H, :], in_=lk.rearrange("b h e -> (b h) e"))
             elif item[0] == "x":
                 load_x(item[1], item[2])
             else:
@@ -88,6 +89,14 @@ def tile_ia3mixedtaskkeyattentionlift_x1_kernel(tc, x, wq, wk, lk, out, words, s
         make_identity(nc, ident[:])
         ident_bf = keep.tile([P, P], BF16, align_bytes=64)
         nc.gpsimd.tensor_copy(out=ident_bf[:], in_=ident[:])
+        lk_t = keep.tile([P, PACK, B * H], F32)
+
+        def lk_turn():
+            bank = psum.tile([P, PACK, P], BF16, name="aux", bufs=BANKS["aux"])
+            for t in range(PACK):
+                nc.tensor.transpose(bank[:, t, :], lk_rows[:, t : E : PACK], ident_bf[:])
+            nc.scalar.copy(out=lk_t[:], in_=bank[:, :, 0 : B * H])
+
         warm = keep.tile([P, 1], F32)
         nc.vector.memset(warm[:], 0.0)
         warm_out = keep.tile([P, 1], F32)
@@ -98,7 +107,6 @@ def tile_ia3mixedtaskkeyattentionlift_x1_kernel(tc, x, wq, wk, lk, out, words, s
         x_bank = {}
         x_mid = {}
         w_mid = {}
-        w_bank = {}
 
         def x_turn(b, c):
             pairs = x_raw[b, c][:].bitcast(F32)
@@ -131,27 +139,11 @@ def tile_ia3mixedtaskkeyattentionlift_x1_kernel(tc, x, wq, wk, lk, out, words, s
                 w_mid[n, h, g] = work.tile([P, PACK, P * PACK], BF16, name="w_mid", bufs=6, align_bytes=64)
             return w_mid[n, h, g]
 
-        def w_source(n, h, g):
-            return w_raw[n, h, g][:].rearrange("p j (m t) -> p t m j", t=PACK)
-
-        def w_turn(n, h, g, half):
-            src = w_source(n, h, g)
-            bank = psum.tile([P, 2, P * PACK], BF16, name="aux", bufs=BANKS["aux"])
-            for i in range(2):
-                nc.tensor.matmul(
-                    bank[:, i, :].rearrange("p (m j) -> p m j", j=PACK), lhsT=ident_bf[:], rhs=src[:, 2 * half + i], start=True, stop=True
-                )
-            w_bank[n, h, g, half] = bank
-
         def w_interleave(n, h, g, half):
-            how = WAY[n, h, g, half]
-            dst = w_target(n, h, g)[:, 2 * half : 2 * half + 2, :]
-            if how in ("TS", "TV"):
-                (nc.scalar.copy if how == "TS" else nc.vector.tensor_copy)(out=dst, in_=w_bank[n, h, g, half][:])
-            else:
-                (nc.scalar.copy if how == "S" else nc.vector.tensor_copy)(
-                    out=dst.rearrange("p t (m j) -> p t m j", j=PACK), in_=w_source(n, h, g)[:, 2 * half : 2 * half + 2]
-                )
+            cols = slice(64 * half, 64 * half + 64)
+            dst = w_target(n, h, g)[:].rearrange("p t (m j) -> p m j t", j=PACK)[:, cols]
+            src = w_raw[n, h, g][:].rearrange("p j (m t) -> p m j t", t=PACK)[:, cols]
+            (nc.scalar.copy if WAY[n, h, g, half] == "S" else nc.vector.tensor_copy)(out=dst, in_=src)
 
         def w_quant(n, h, g):
             codes = keep.tile([P, E], U32, name=f"w_codes_{n}{h}{g}", align_bytes=64)
@@ -187,8 +179,8 @@ def tile_ia3mixedtaskkeyattentionlift_x1_kernel(tc, x, wq, wk, lk, out, words, s
 
         def q_out(u, c):
             nc.scalar.copy(
-                out=st["qg", u][:, :, 32 * c : 32 * (c + 1), :],
-                in_=st["q", u, c][:].rearrange("p j (m t) -> p t m j", t=PACK),
+                out=st["qg", u][:, :, 32 * c : 32 * (c + 1), :].rearrange("p t m j -> p m t j"),
+                in_=st["q", u, c][:].rearrange("p j (m t) -> p m t j", t=PACK),
             )
 
         def k_out(u, c):
@@ -196,7 +188,7 @@ def tile_ia3mixedtaskkeyattentionlift_x1_kernel(tc, x, wq, wk, lk, out, words, s
             nc.vector.tensor_mul(
                 out=st["kg", u][:, c * P : (c + 1) * P, :],
                 in0=st["k", u, c][:].rearrange("p j r -> p r j"),
-                in1=lk_t[:, b * H + h, :].unsqueeze(1).to_broadcast([P, P, PACK]),
+                in1=lk_t[:, :, b * H + h].unsqueeze(1).to_broadcast([P, P, PACK]),
             )
 
         def quantise(grouped, name):
@@ -279,8 +271,9 @@ def tile_ia3mixedtaskkeyattentionlift_x1_kernel(tc, x, wq, wk, lk, out, words, s
             cols = slice(i * n, i * n + n)
             grouped = work.tile([P, n, PACK], BF16, name=f"p_grouped{parts}", bufs=3, align_bytes=64)
             st["pg", u, i] = grouped
-            src = st["o", u][:, :, cols].rearrange("p t k -> p k t")
-            (nc.vector.tensor_copy if PI[u][i] == "V" else nc.scalar.copy)(out=grouped[:], in_=src)
+            src = st["o", u][:, :, cols].rearrange("p t (k i) -> p k t i", i=4)
+            dst = grouped[:].rearrange("p (k i) t -> p k t i", i=4)
+            (nc.vector.tensor_copy if PI[u][i] == "V" else nc.scalar.copy)(out=dst, in_=src)
 
         def p_quant(u, i):
             b, h = UNITS[u]
@@ -310,7 +303,7 @@ def tile_ia3mixedtaskkeyattentionlift_x1_kernel(tc, x, wq, wk, lk, out, words, s
             (q_out if n == "q" else k_out)(u, c)
 
         steps = {
-            "xt": x_turn, "xc": x_copy, "xq": x_quant, "wt": w_turn, "wi": w_interleave, "wq": w_quant,
+            "lk": lk_turn, "xt": x_turn, "xc": x_copy, "xq": x_quant, "wi": w_interleave, "wq": w_quant,
             "p": project, "ev": evacuate, "qz": lambda n, u: (q_quant if n == "q" else k_quant)(u),
             "z": score, "mx": row_max, "nb": row_bias, "ex": row_exp, "inv": inverse, "rc": row_inverse,
             "sc": row_scale, "pi": p_group, "pq": p_quant,

@@ -23,29 +23,29 @@ G = D // 512
 NC = S // P
 SCALE = 1.0 / math.sqrt(E)
 UNITS = [(0, 0), (1, 0), (0, 1), (1, 1)]
-BANKS = {'aux': 2, 'proj': 3, 'z': 3}
-LOADS = [('x', 1, 2), ('k', 0, 1), ('k', 0, 0), ('x', 0, 1), ('x', 0, 0), ('q', 0, 1), ('lk',), ('x', 0, 2), ('q', 0, 0), ('x', 1, 3), ('q', 1, 0), ('x', 0, 3), ('q', 1, 1), ('k', 1, 0), ('x', 1, 0), ('x', 1, 1), ('k', 1, 1)]
-WAY = {('k', 0, 0, 0): 'S', ('k', 0, 0, 1): 'V', ('k', 0, 1, 0): 'S', ('k', 0, 1, 1): 'V', ('k', 1, 0, 0): 'S', ('k', 1, 0, 1): 'S', ('k', 1, 1, 0): 'S', ('k', 1, 1, 1): 'V', ('q', 0, 0, 0): 'V', ('q', 0, 0, 1): 'S', ('q', 0, 1, 0): 'S', ('q', 0, 1, 1): 'V', ('q', 1, 0, 0): 'V', ('q', 1, 0, 1): 'S', ('q', 1, 1, 0): 'V', ('q', 1, 1, 1): 'S'}
+BANKS = {'all': 8}
+LOADS = [('x', 0, 0), ('k', 0, 1), ('k', 0, 0), ('q', 0, 0), ('x', 0, 3), ('q', 0, 1), ('x', 0, 2), ('x', 1, 3), ('lk',), ('x', 0, 1), ('k', 1, 0), ('x', 1, 1), ('k', 1, 1), ('x', 1, 2), ('q', 1, 0), ('q', 1, 1), ('x', 1, 0)]
+WAY = {('k', 0, 0, 0): 'V', ('k', 0, 0, 1): 'S', ('k', 0, 1, 0): 'V', ('k', 0, 1, 1): 'S', ('k', 1, 0, 0): 'V', ('k', 1, 0, 1): 'S', ('k', 1, 1, 0): 'V', ('k', 1, 1, 1): 'S', ('q', 0, 0, 0): 'V', ('q', 0, 0, 1): 'S', ('q', 0, 1, 0): 'V', ('q', 0, 1, 1): 'S', ('q', 1, 0, 0): 'S', ('q', 1, 0, 1): 'S', ('q', 1, 1, 0): 'V', ('q', 1, 1, 1): 'S'}
 SC = ['SSSS', 'SSSS', 'VVVV', 'VVVV']
-PI = ['S', 'VS', 'VS', 'VS']
-XC = ['S', 'S', 'S', 'V', 'V', 'S', 'V', 'S']
+PI = ['VS', 'VS', 'VS', 'VS']
+XC = ['V', 'S', 'S', 'S', 'S', 'S', 'S', 'S']
 ORDER = (
-    "xt.1.2 xc.1.2 wi.k.0.1.0 wi.k.0.1.1 xq.1.2 wi.k.0.0.1 wi.k.0.0.0 xt.0.1 wq.k.0.1 xt.0.0 xc.0.1 wq.k.0.0 xc.0.0 "
-    "xq.0.1 lk p.k.1.2 wi.q.0.1.1 wi.q.0.1.0 p.k.0.1 xq.0.0 ev.k.1.2 p.k.0.0 wq.q.0.1 wi.q.0.0.1 xt.0.2 wi.q.0.0.0 "
-    "xt.1.3 ev.k.0.1 xc.0.2 wq.q.0.0 wi.q.1.0.1 xt.0.3 xq.0.2 ev.k.0.0 p.q.0.2 xc.1.3 xc.0.3 p.q.0.0 wi.q.1.1.1 "
-    "wi.q.1.1.0 p.k.0.2 xq.0.3 xq.1.3 ev.q.0.2 wq.q.1.1 xt.1.0 ev.q.0.0 ev.k.0.2 p.q.0.1 wi.k.1.0.0 wi.q.1.0.0 "
-    "p.k.0.3 xc.1.0 p.q.0.3 ev.q.0.1 ev.k.0.3 xt.1.1 wi.k.1.0.1 xq.1.0 qz.k.0 p.q.1.3 wq.q.1.0 ev.q.0.3 p.k.1.3 "
-    "wi.k.1.1.1 ev.q.1.3 p.q.1.2 xc.1.1 qz.q.0 p.q.1.0 ev.q.1.2 ev.k.1.3 z.0.1 ev.q.1.0 xq.1.1 z.0.2 mx.0.1 z.0.0 "
-    "wi.k.1.1.0 p.q.1.1 mx.0.0 p.k.1.1 mx.0.2 ev.q.1.1 p.k.1.0 nb.0.0 ev.k.1.1 ex.0.0 p.q.2.1 qz.q.1 ex.0.1 z.0.3 "
-    "ev.k.1.0 p.q.2.3 ev.q.2.1 mx.0.3 p.q.2.0 ev.q.2.3 qz.k.1 p.q.2.2 ev.q.2.0 nb.0.1 wq.k.1.1 z.1.3 ex.0.2 p.q.3.3 "
-    "wq.k.1.0 ex.0.3 mx.1.3 z.1.2 p.k.2.1 ev.q.2.2 inv.0 mx.1.2 z.1.0 sc.0.2 p.k.2.3 ev.k.2.1 ev.q.3.3 nb.1.1 "
-    "mx.1.0 p.k.2.0 ex.1.3 ev.k.2.3 p.k.2.2 ex.1.2 ev.k.2.0 z.1.1 sc.0.1 p.q.3.2 ev.k.2.2 sc.0.3 p.k.3.3 mx.1.1 "
-    "sc.0.0 qz.k.2 p.q.3.0 ev.q.3.2 nb.1.0 qz.q.2 ex.1.1 p.k.3.1 ev.k.3.3 ex.1.0 z.2.2 ev.k.3.1 z.2.0 ev.q.3.0 "
-    "p.k.3.2 mx.2.2 pi.0.0 z.2.1 mx.2.0 p.k.3.0 mx.2.1 p.q.3.1 inv.1 nb.2.0 ev.k.3.2 ev.k.3.0 ex.2.0 pq.0.0 "
-    "ev.q.3.1 z.2.3 qz.k.3 ex.2.1 mx.2.3 sc.1.2 rc.2.1 rc.2.0 nb.2.1 qz.q.3 ex.2.3 sc.2.1 z.3.1 ex.2.2 sc.2.0 z.3.3 "
-    "mx.3.1 sc.1.0 z.3.0 mx.3.3 sc.1.3 mx.3.0 sc.1.1 rc.2.3 rc.2.2 nb.3.0 sc.2.3 ex.3.0 sc.2.2 pi.1.0 ex.3.1 z.3.2 "
-    "mx.3.2 pi.2.1 pq.1.0 nb.3.1 rc.3.0 rc.3.1 pi.2.0 ex.3.3 pq.2.1 ex.3.2 pq.2.0 sc.3.1 pi.1.1 rc.3.3 rc.3.2 "
-    "sc.3.0 sc.3.2 sc.3.3 pi.3.1 pi.3.0 pq.1.1 pq.3.0 pq.3.1 "
+    "xt.0.0 xc.0.0 wi.k.0.1.1 wi.k.0.1.0 xq.0.0 wi.k.0.0.0 wi.k.0.0.1 wq.k.0.1 wi.q.0.0.0 wi.q.0.0.1 xt.0.3 "
+    "wq.k.0.0 xc.0.3 lk p.k.0.0 wq.q.0.0 wi.q.0.1.1 xq.0.3 xt.0.2 wi.q.0.1.0 xt.1.3 ev.k.0.0 xc.0.2 xt.0.1 wq.q.0.1 "
+    "xc.1.3 p.k.0.3 xq.0.2 xc.0.1 xq.1.3 p.k.0.2 ev.k.0.3 wi.k.1.0.1 p.q.0.2 xq.0.1 ev.k.0.2 p.q.0.0 ev.q.0.2 "
+    "wi.k.1.1.0 p.k.0.1 wi.k.1.1.1 wi.k.1.0.0 p.q.0.3 ev.k.0.1 xt.1.2 ev.q.0.0 wq.k.1.1 ev.q.0.3 xt.1.1 qz.k.0 "
+    "xc.1.2 p.q.0.1 wq.k.1.0 xc.1.1 xt.1.0 xq.1.2 ev.q.0.1 wi.q.1.1.0 p.k.1.3 xc.1.0 qz.q.0 p.q.1.3 wi.q.1.0.1 "
+    "ev.k.1.3 z.0.3 xq.1.1 z.0.0 mx.0.3 z.0.1 ev.q.1.3 z.0.2 mx.0.1 p.k.1.1 wi.q.1.1.1 mx.0.2 p.k.1.2 mx.0.0 "
+    "p.q.1.2 wi.q.1.0.0 nb.0.1 ev.k.1.2 p.k.2.3 nb.0.0 xq.1.0 p.k.2.2 ex.0.1 ev.k.1.1 ex.0.2 wq.q.1.0 p.q.1.0 "
+    "ex.0.0 wq.q.1.1 p.k.1.0 ev.k.2.2 ev.q.1.2 p.k.2.1 ev.k.1.0 ex.0.3 p.q.2.3 ev.k.2.1 ev.q.1.0 p.q.1.1 qz.k.1 "
+    "ev.q.2.3 p.k.2.0 inv.0 ev.q.1.1 ev.k.2.3 p.k.3.0 sc.0.2 ev.k.2.0 p.k.3.3 sc.0.0 qz.q.1 p.q.2.1 sc.0.1 qz.k.2 "
+    "z.1.3 sc.0.3 ev.k.3.0 z.1.2 z.1.1 ev.q.2.1 mx.1.3 z.1.0 p.q.2.2 pi.0.1 mx.1.0 p.q.3.3 mx.1.1 p.k.3.1 mx.1.2 "
+    "ev.q.2.2 nb.1.0 ev.q.3.3 pq.0.1 p.q.3.0 nb.1.1 pi.0.0 ex.1.0 p.q.2.0 ev.k.3.1 ex.1.2 p.k.3.2 pq.0.0 ev.q.3.0 "
+    "ev.k.3.3 p.q.3.1 ev.q.2.0 ev.k.3.2 p.q.3.2 ex.1.1 qz.q.2 ex.1.3 qz.k.3 z.2.1 z.2.2 ev.q.3.1 mx.2.1 z.2.3 z.2.0 "
+    "ev.q.3.2 inv.1 mx.2.2 sc.1.0 qz.q.3 sc.1.3 mx.2.0 z.3.1 sc.1.1 z.3.0 mx.2.3 z.3.3 sc.1.2 z.3.2 nb.2.0 mx.3.0 "
+    "ex.2.1 nb.2.1 mx.3.3 ex.2.3 rc.2.1 mx.3.2 ex.2.0 sc.2.1 ex.2.2 nb.3.1 rc.2.3 rc.2.0 mx.3.1 ex.3.2 sc.2.3 "
+    "sc.2.0 ex.3.3 nb.3.0 rc.2.2 rc.3.2 pi.1.0 ex.3.1 sc.2.2 ex.3.0 sc.3.2 pq.1.0 pi.2.1 rc.3.3 rc.3.1 rc.3.0 "
+    "sc.3.3 sc.3.1 sc.3.0 pi.2.0 pi.1.1 pq.2.1 pq.2.0 pi.3.0 pi.3.1 pq.1.1 pq.3.0 pq.3.1 "
 ).split()
 
 
@@ -89,13 +89,13 @@ def tile_ia3mixedtaskkeyattentionlift_x1_kernel(tc, x, wq, wk, lk, out, words, s
         make_identity(nc, ident[:])
         ident_bf = keep.tile([P, P], BF16, align_bytes=64)
         nc.gpsimd.tensor_copy(out=ident_bf[:], in_=ident[:])
-        lk_t = keep.tile([P, PACK, B * H], F32)
+        lk_t = keep.tile([P, B * H, PACK], F32, align_bytes=64)
 
         def lk_turn():
-            bank = psum.tile([P, PACK, P], BF16, name="aux", bufs=BANKS["aux"])
+            bank = psum.tile([P, PACK, P], BF16, name="aux", tag="bank", bufs=8)
             for t in range(PACK):
                 nc.tensor.transpose(bank[:, t, :], lk_rows[:, t : E : PACK], ident_bf[:])
-            nc.scalar.copy(out=lk_t[:], in_=bank[:, :, 0 : B * H])
+            nc.scalar.copy(out=lk_t[:], in_=bank[:, :, 0 : B * H].rearrange("p t b -> p b t"))
 
         warm = keep.tile([P, 1], F32)
         nc.vector.memset(warm[:], 0.0)
@@ -104,13 +104,14 @@ def tile_ia3mixedtaskkeyattentionlift_x1_kernel(tc, x, wq, wk, lk, out, words, s
 
         x_q = {}
         w_q = {}
+        w_bank = {}
         x_bank = {}
         x_mid = {}
         w_mid = {}
 
         def x_turn(b, c):
             pairs = x_raw[b, c][:].bitcast(F32)
-            bank = psum.tile([P, G * 2, P], F32, name="aux", bufs=BANKS["aux"])
+            bank = psum.tile([P, G * 2, P], F32, name="aux", tag="bank", bufs=8)
             for g in range(G):
                 for u in range(2):
                     nc.tensor.transpose(bank[:, 2 * g + u, :], pairs[:, 256 * g + u : 256 * (g + 1) : 2], ident[:])
@@ -139,7 +140,21 @@ def tile_ia3mixedtaskkeyattentionlift_x1_kernel(tc, x, wq, wk, lk, out, words, s
                 w_mid[n, h, g] = work.tile([P, PACK, P * PACK], BF16, name="w_mid", bufs=6, align_bytes=64)
             return w_mid[n, h, g]
 
+        def w_turn(n, h, g, half):
+            bank = psum.tile([P, PACK, 64, PACK], BF16, name="aux", tag="bank", bufs=8)
+            src = w_raw[n, h, g][:].rearrange("p (a b) (m t) -> p a m t b", b=2, t=PACK)
+            dst = bank[:].rearrange("p t m (a b) -> p a m t b", b=2)
+            for a in range(2):
+                nc.tensor.matmul(dst[:, a], lhsT=ident_bf[:], rhs=src[:, a, 64 * half : 64 * half + 64], start=True, stop=True)
+            w_bank[n, h, g, half] = bank
+
         def w_interleave(n, h, g, half):
+            if WAY[n, h, g, half] == "TS":
+                nc.scalar.copy(
+                    out=w_target(n, h, g)[:, :, 256 * half : 256 * half + 256],
+                    in_=w_bank[n, h, g, half][:].rearrange("p t m j -> p t (m j)"),
+                )
+                return
             cols = slice(64 * half, 64 * half + 64)
             dst = w_target(n, h, g)[:].rearrange("p t (m j) -> p m j t", j=PACK)[:, cols]
             src = w_raw[n, h, g][:].rearrange("p j (m t) -> p m j t", t=PACK)[:, cols]
@@ -154,10 +169,11 @@ def tile_ia3mixedtaskkeyattentionlift_x1_kernel(tc, x, wq, wk, lk, out, words, s
             w_q[n, h, g] = (codes, scl)
 
         st = {}
+        p_scales = keep.tile([P, S], U8, align_bytes=64)
 
         def project(n, u, c):
             b, h = UNITS[u]
-            bank = psum.tile([P, PACK, P], F32, name="proj", bufs=BANKS["proj"])
+            bank = psum.tile([P, PACK, P], F32, name="proj", tag="bank", bufs=8)
             x_codes, x_scl = x_q[b, c]
             for t in range(PACK):
                 for g in range(G):
@@ -179,8 +195,8 @@ def tile_ia3mixedtaskkeyattentionlift_x1_kernel(tc, x, wq, wk, lk, out, words, s
 
         def q_out(u, c):
             nc.scalar.copy(
-                out=st["qg", u][:, :, 32 * c : 32 * (c + 1), :].rearrange("p t m j -> p m t j"),
-                in_=st["q", u, c][:].rearrange("p j (m t) -> p m t j", t=PACK),
+                out=st["qg", u][:, :, 32 * c : 32 * (c + 1), :],
+                in_=st["q", u, c][:].rearrange("p j (m t) -> p t m j", t=PACK),
             )
 
         def k_out(u, c):
@@ -188,7 +204,7 @@ def tile_ia3mixedtaskkeyattentionlift_x1_kernel(tc, x, wq, wk, lk, out, words, s
             nc.vector.tensor_mul(
                 out=st["kg", u][:, c * P : (c + 1) * P, :],
                 in0=st["k", u, c][:].rearrange("p j r -> p r j"),
-                in1=lk_t[:, :, b * H + h].unsqueeze(1).to_broadcast([P, P, PACK]),
+                in1=lk_t[:, b * H + h, :].unsqueeze(1).to_broadcast([P, P, PACK]),
             )
 
         def quantise(grouped, name):
@@ -214,7 +230,7 @@ def tile_ia3mixedtaskkeyattentionlift_x1_kernel(tc, x, wq, wk, lk, out, words, s
                 open_scores(u)
             q_codes, q_scl = st["Q", u]
             k_codes, k_scl = st["K", u]
-            z = psum.tile([P, S], F32, name="z", bufs=BANKS["z"])
+            z = psum.tile([P, S], F32, name="z", tag="bank", bufs=8)
             nc.tensor.matmul_mx(
                 out=z[:],
                 lhsT=q_codes[:, t * P : (t + 1) * P].bitcast(FP8X4),
@@ -281,21 +297,23 @@ def tile_ia3mixedtaskkeyattentionlift_x1_kernel(tc, x, wq, wk, lk, out, words, s
             n = S // parts
             if ("pc", u) not in st:
                 st["pc", u] = work.tile([P, S], U32, name="p_codes", bufs=3, align_bytes=64)
-                st["ps", u] = work.tile([P, S], U8, name="p_scales", bufs=3, align_bytes=64)
-            codes, scl = st["pc", u], st["ps", u]
+            codes = st["pc", u]
+            first_row = 4 * (b * H + h)
             cols = slice(i * n, i * n + n)
             nc.vector.quantize_mx(
-                out=codes[:, cols].bitcast(FP8X4), scales=scl[:, cols], in_=st["pg", u, i][:].rearrange("p k t -> p (k t)")
+                out=codes[:, cols].bitcast(FP8X4), scales=p_scales[first_row:P, cols], in_=st["pg", u, i][:].rearrange("p k t -> p (k t)")
             )
             left["pq", u] = left.get(("pq", u), 0) + 1
             if left["pq", u] == parts:
                 col = (b * H + h) * S
                 nc.sync.dma_start(out=words32[:, col : col + S], in_=codes[:].bitcast(I32))
-                for quad in range(4):
-                    nc.sync.dma_start(
-                        out=scales32[4 * quad : 4 * quad + 4, col // 4 : (col + S) // 4],
-                        in_=scl[32 * quad : 32 * quad + 4, :].bitcast(I32),
-                    )
+                left["all"] = left.get("all", 0) + 1
+                if left["all"] == B * H:
+                    for quad in range(4):
+                        nc.sync.dma_start(
+                            out=scales32[4 * quad : 4 * quad + 4, :].rearrange("r (u m) -> u r m", u=B * H),
+                            in_=p_scales[32 * quad : 32 * quad + 16, :].bitcast(I32),
+                        )
 
         def evacuate(n, u, c):
             if ("qg", u) not in st:
@@ -303,7 +321,7 @@ def tile_ia3mixedtaskkeyattentionlift_x1_kernel(tc, x, wq, wk, lk, out, words, s
             (q_out if n == "q" else k_out)(u, c)
 
         steps = {
-            "lk": lk_turn, "xt": x_turn, "xc": x_copy, "xq": x_quant, "wi": w_interleave, "wq": w_quant,
+            "lk": lk_turn, "xt": x_turn, "xc": x_copy, "xq": x_quant, "wt": w_turn, "wi": w_interleave, "wq": w_quant,
             "p": project, "ev": evacuate, "qz": lambda n, u: (q_quant if n == "q" else k_quant)(u),
             "z": score, "mx": row_max, "nb": row_bias, "ex": row_exp, "inv": inverse, "rc": row_inverse,
             "sc": row_scale, "pi": p_group, "pq": p_quant,

import math
from contextlib import ExitStack

import concourse.mybir as mybir
from concourse.masks import make_identity

B, S, D, H, E = 2, 512, 1024, 2, 512
FLOPS = 2 * B * H * (2 * S * D * E + S * S * E)

F32 = mybir.dt.float32
BF16 = mybir.dt.bfloat16
U32 = mybir.dt.uint32
I32 = mybir.dt.int32
U8 = mybir.dt.uint8
FP8X4 = mybir.dt.float8_e4m3fn_x4
ALU = mybir.AluOpType
ACT = mybir.ActivationFunctionType
AX = mybir.AxisListType

P = 128
PACK = 4
G = D // 512
NC = S // P
SCALE = 1.0 / math.sqrt(E)
UNITS = [(0, 0), (1, 0), (0, 1), (1, 1)]
BANKS = {'all': 8}
LOADS = [('x', 0, 0), ('k', 0, 1), ('k', 0, 0), ('q', 0, 0), ('x', 0, 3), ('q', 0, 1), ('x', 0, 2), ('x', 1, 3), ('lk',), ('x', 0, 1), ('k', 1, 0), ('x', 1, 1), ('k', 1, 1), ('x', 1, 2), ('q', 1, 0), ('q', 1, 1), ('x', 1, 0)]
WAY = {('k', 0, 0, 0): 'V', ('k', 0, 0, 1): 'S', ('k', 0, 1, 0): 'V', ('k', 0, 1, 1): 'S', ('k', 1, 0, 0): 'V', ('k', 1, 0, 1): 'S', ('k', 1, 1, 0): 'V', ('k', 1, 1, 1): 'S', ('q', 0, 0, 0): 'V', ('q', 0, 0, 1): 'S', ('q', 0, 1, 0): 'V', ('q', 0, 1, 1): 'S', ('q', 1, 0, 0): 'S', ('q', 1, 0, 1): 'S', ('q', 1, 1, 0): 'V', ('q', 1, 1, 1): 'S'}
SC = ['SSSS', 'SSSS', 'VVVV', 'VVVV']
PI = ['VS', 'VS', 'VS', 'VS']
XC = ['V', 'S', 'S', 'S', 'S', 'S', 'S', 'S']
ORDER = (
    "xt.0.0 xc.0.0 wi.k.0.1.1 wi.k.0.1.0 xq.0.0 wi.k.0.0.0 wi.k.0.0.1 wq.k.0.1 wi.q.0.0.0 wi.q.0.0.1 xt.0.3 "
    "wq.k.0.0 xc.0.3 lk p.k.0.0 wq.q.0.0 wi.q.0.1.1 xq.0.3 xt.0.2 wi.q.0.1.0 xt.1.3 ev.k.0.0 xc.0.2 xt.0.1 wq.q.0.1 "
    "xc.1.3 p.k.0.3 xq.0.2 xc.0.1 xq.1.3 p.k.0.2 ev.k.0.3 wi.k.1.0.1 p.q.0.2 xq.0.1 ev.k.0.2 p.q.0.0 ev.q.0.2 "
    "wi.k.1.1.0 p.k.0.1 wi.k.1.1.1 wi.k.1.0.0 p.q.0.3 ev.k.0.1 xt.1.2 ev.q.0.0 wq.k.1.1 ev.q.0.3 xt.1.1 qz.k.0 "
    "xc.1.2 p.q.0.1 wq.k.1.0 xc.1.1 xt.1.0 xq.1.2 ev.q.0.1 wi.q.1.1.0 p.k.1.3 xc.1.0 qz.q.0 p.q.1.3 wi.q.1.0.1 "
    "ev.k.1.3 z.0.3 xq.1.1 z.0.0 mx.0.3 z.0.1 ev.q.1.3 z.0.2 mx.0.1 p.k.1.1 wi.q.1.1.1 mx.0.2 p.k.1.2 mx.0.0 "
    "p.q.1.2 wi.q.1.0.0 nb.0.1 ev.k.1.2 p.k.2.3 nb.0.0 xq.1.0 p.k.2.2 ex.0.1 ev.k.1.1 ex.0.2 wq.q.1.0 p.q.1.0 "
    "ex.0.0 wq.q.1.1 p.k.1.0 ev.k.2.2 ev.q.1.2 p.k.2.1 ev.k.1.0 ex.0.3 p.q.2.3 ev.k.2.1 ev.q.1.0 p.q.1.1 qz.k.1 "
    "ev.q.2.3 p.k.2.0 inv.0 ev.q.1.1 ev.k.2.3 p.k.3.0 sc.0.2 ev.k.2.0 p.k.3.3 sc.0.0 qz.q.1 p.q.2.1 sc.0.1 qz.k.2 "
    "z.1.3 sc.0.3 ev.k.3.0 z.1.2 z.1.1 ev.q.2.1 mx.1.3 z.1.0 p.q.2.2 pi.0.1 mx.1.0 p.q.3.3 mx.1.1 p.k.3.1 mx.1.2 "
    "ev.q.2.2 nb.1.0 ev.q.3.3 pq.0.1 p.q.3.0 nb.1.1 pi.0.0 ex.1.0 p.q.2.0 ev.k.3.1 ex.1.2 p.k.3.2 pq.0.0 ev.q.3.0 "
    "ev.k.3.3 p.q.3.1 ev.q.2.0 ev.k.3.2 p.q.3.2 ex.1.1 qz.q.2 ex.1.3 qz.k.3 z.2.1 z.2.2 ev.q.3.1 mx.2.1 z.2.3 z.2.0 "
    "ev.q.3.2 inv.1 mx.2.2 sc.1.0 qz.q.3 sc.1.3 mx.2.0 z.3.1 sc.1.1 z.3.0 mx.2.3 z.3.3 sc.1.2 z.3.2 nb.2.0 mx.3.0 "
    "ex.2.1 nb.2.1 mx.3.3 ex.2.3 rc.2.1 mx.3.2 ex.2.0 sc.2.1 ex.2.2 nb.3.1 rc.2.3 rc.2.0 mx.3.1 ex.3.2 sc.2.3 "
    "sc.2.0 ex.3.3 nb.3.0 rc.2.2 rc.3.2 pi.1.0 ex.3.1 sc.2.2 ex.3.0 sc.3.2 pq.1.0 pi.2.1 rc.3.3 rc.3.1 rc.3.0 "
    "sc.3.3 sc.3.1 sc.3.0 pi.2.0 pi.1.1 pq.2.1 pq.2.0 pi.3.0 pi.3.1 pq.1.1 pq.3.0 pq.3.1 "
).split()


def tile_ia3mixedtaskkeyattentionlift_x1_kernel(tc, x, wq, wk, lk, out, words, scales):
    nc = tc.nc
    words32 = words.rearrange("g p m t -> (g p) (m t)").bitcast(I32)
    scales32 = scales.rearrange("g q m -> (g q) m").bitcast(I32)

    with ExitStack() as ctx:
        keep = ctx.enter_context(tc.tile_pool(name="keep", bufs=1))
        load = ctx.enter_context(tc.tile_pool(name="load", bufs=8))
        work = ctx.enter_context(tc.tile_pool(name="work", bufs=2))
        psum = ctx.enter_context(tc.psum_pool(name="psum", bufs=2))
        ctx.enter_context(tc.manual_schedule())

        x_raw = {}
        w_raw = {}
        w_in = {"q": wq, "k": wk}

        def load_x(b, c):
            t = load.tile([P, D], BF16, name="x_rows", align_bytes=64)
            nc.sync.dma_start(out=t[:], in_=x[b, c * P : (c + 1) * P, :])
            x_raw[b, c] = t

        def load_w(n, h, g):
            t = load.tile([P, PACK, E], BF16, name="w_rows", align_bytes=64)
            nc.sync.dma_start(out=t[:], in_=w_in[n][h, g * 512 : (g + 1) * 512, :].rearrange("(p j) w -> p j w", j=PACK))
            w_raw[n, h, g] = t

        lk_rows = keep.tile([P, E], BF16, align_bytes=64)
        nc.gpsimd.memset(lk_rows[:], 0.0)
        for item in LOADS:
            if item[0] == "lk":
                nc.sync.dma_start(out=lk_rows[0 : B * H, :], in_=lk.rearrange("b h e -> (b h) e"))
            elif item[0] == "x":
                load_x(item[1], item[2])
            else:
                load_w(item[0], item[1], item[2])

        ident = keep.tile([P, P], F32, align_bytes=64)
        make_identity(nc, ident[:])
        ident_bf = keep.tile([P, P], BF16, align_bytes=64)
        nc.gpsimd.tensor_copy(out=ident_bf[:], in_=ident[:])
        lk_t = keep.tile([P, B * H, PACK], F32, align_bytes=64)

        def lk_turn():
            bank = psum.tile([P, PACK, P], BF16, name="aux", tag="bank", bufs=8)
            for t in range(PACK):
                nc.tensor.transpose(bank[:, t, :], lk_rows[:, t : E : PACK], ident_bf[:])
            nc.scalar.copy(out=lk_t[:], in_=bank[:, :, 0 : B * H].rearrange("p t b -> p b t"))

        warm = keep.tile([P, 1], F32)
        nc.vector.memset(warm[:], 0.0)
        warm_out = keep.tile([P, 1], F32)
        nc.scalar.activation(out=warm_out[:], in_=warm[:], func=ACT.Exp)

        x_q = {}
        w_q = {}
        w_bank = {}
        x_bank = {}
        x_mid = {}
        w_mid = {}

        def x_turn(b, c):
            pairs = x_raw[b, c][:].bitcast(F32)
            bank = psum.tile([P, G * 2, P], F32, name="aux", tag="bank", bufs=8)
            for g in range(G):
                for u in range(2):
                    nc.tensor.transpose(bank[:, 2 * g + u, :], pairs[:, 256 * g + u : 256 * (g + 1) : 2], ident[:])
            x_bank[b, c] = bank

        def x_copy(b, c):
            grouped = work.tile([P, G, P, PACK], BF16, name="x_grouped", bufs=8, align_bytes=64)
            (nc.scalar.copy if XC[4 * b + c] == "S" else nc.vector.tensor_copy)(
                out=grouped[:].bitcast(F32),
                in_=x_bank[b, c][:].rearrange("p (g u) r -> p g r u", u=2),
            )
            x_mid[b, c] = grouped

        def x_quant(b, c):
            codes = keep.tile([P, G, P], U32, name=f"x_codes_{b}{c}", align_bytes=64)
            scl = keep.tile([P, G, P], U8, name=f"x_scales_{b}{c}", align_bytes=64)
            nc.vector.quantize_mx(
                out=codes[:].rearrange("p g r -> p (g r)").bitcast(FP8X4),
                scales=scl[:].rearrange("p g r -> p (g r)"),
                in_=x_mid[b, c][:].rearrange("p g r j -> p (g r j)"),
            )
            x_q[b, c] = (codes, scl)

        def w_target(n, h, g):
            if (n, h, g) not in w_mid:
                w_mid[n, h, g] = work.tile([P, PACK, P * PACK], BF16, name="w_mid", bufs=6, align_bytes=64)
            return w_mid[n, h, g]

        def w_turn(n, h, g, half):
            bank = psum.tile([P, PACK, 64, PACK], BF16, name="aux", tag="bank", bufs=8)
            src = w_raw[n, h, g][:].rearrange("p (a b) (m t) -> p a m t b", b=2, t=PACK)
            dst = bank[:].rearrange("p t m (a b) -> p a m t b", b=2)
            for a in range(2):
                nc.tensor.matmul(dst[:, a], lhsT=ident_bf[:], rhs=src[:, a, 64 * half : 64 * half + 64], start=True, stop=True)
            w_bank[n, h, g, half] = bank

        def w_interleave(n, h, g, half):
            if WAY[n, h, g, half] == "TS":
                nc.scalar.copy(
                    out=w_target(n, h, g)[:, :, 256 * half : 256 * half + 256],
                    in_=w_bank[n, h, g, half][:].rearrange("p t m j -> p t (m j)"),
                )
                return
            cols = slice(64 * half, 64 * half + 64)
            dst = w_target(n, h, g)[:].rearrange("p t (m j) -> p m j t", j=PACK)[:, cols]
            src = w_raw[n, h, g][:].rearrange("p j (m t) -> p m j t", t=PACK)[:, cols]
            (nc.scalar.copy if WAY[n, h, g, half] == "S" else nc.vector.tensor_copy)(out=dst, in_=src)

        def w_quant(n, h, g):
            codes = keep.tile([P, E], U32, name=f"w_codes_{n}{h}{g}", align_bytes=64)
            scl = keep.tile([P, E], U8, name=f"w_scales_{n}{h}{g}", align_bytes=64)
            nc.vector.quantize_mx(
                out=codes[:].bitcast(FP8X4), scales=scl[:], in_=w_mid[n, h, g][:].rearrange("p t c -> p (t c)")
            )
            w_q[n, h, g] = (codes, scl)

        st = {}
        p_scales = keep.tile([P, S], U8, align_bytes=64)

        def project(n, u, c):
            b, h = UNITS[u]
            bank = psum.tile([P, PACK, P], F32, name="proj", tag="bank", bufs=8)
            x_codes, x_scl = x_q[b, c]
            for t in range(PACK):
                for g in range(G):
                    w_codes, w_scl = w_q[n, h, g]
                    nc.tensor.matmul_mx(
                        out=bank[:, t, :],
                        lhsT=w_codes[:, t * P : (t + 1) * P].bitcast(FP8X4),
                        lhsT_scale=w_scl[:, t * P : (t + 1) * P],
                        rhs=x_codes[:, g, :].bitcast(FP8X4),
                        rhs_scale=x_scl[:, g, :],
                        start=(g == 0),
                        stop=(g == G - 1),
                    )
            st[n, u, c] = bank

        def open_unit(u):
            st["qg", u] = work.tile([P, PACK, P, PACK], BF16, name="q_grouped", bufs=3, align_bytes=64)
            st["kg", u] = work.tile([P, S, PACK], BF16, name="k_grouped", bufs=3, align_bytes=64)

        def q_out(u, c):
            nc.scalar.copy(
                out=st["qg", u][:, :, 32 * c : 32 * (c + 1), :],
                in_=st["q", u, c][:].rearrange("p j (m t) -> p t m j", t=PACK),
            )

        def k_out(u, c):
            b, h = UNITS[u]
            nc.vector.tensor_mul(
                out=st["kg", u][:, c * P : (c + 1) * P, :],
                in0=st["k", u, c][:].rearrange("p j r -> p r j"),
                in1=lk_t[:, b * H + h, :].unsqueeze(1).to_broadcast([P, P, PACK]),
            )

        def quantise(grouped, name):
            codes = work.tile([P, S], U32, name=name + "_codes", bufs=4, align_bytes=64)
            scl = work.tile([P, S], U8, name=name + "_scales", bufs=4, align_bytes=64)
            nc.vector.quantize_mx(out=codes[:].bitcast(FP8X4), scales=scl[:], in_=grouped)
            return codes, scl

        def q_quant(u):
            st["Q", u] = quantise(st["qg", u][:].rearrange("p t m j -> p (t m j)"), "q")

        def k_quant(u):
            st["K", u] = quantise(st["kg", u][:].rearrange("p r j -> p (r j)"), "k")

        def open_scores(u):
            for n in ("neg", "bias", "total", "inv"):
                st[n, u] = work.tile([P, PACK], F32, name=n, bufs=4)
            st["e", u] = work.tile([P, PACK, S], F32, name="e", bufs=3, align_bytes=64)
            st["o", u] = work.tile([P, PACK, S], F32, name="o", bufs=3, align_bytes=64)

        def score(u, t):
            if ("e", u) not in st:
                open_scores(u)
            q_codes, q_scl = st["Q", u]
            k_codes, k_scl = st["K", u]
            z = psum.tile([P, S], F32, name="z", tag="bank", bufs=8)
            nc.tensor.matmul_mx(
                out=z[:],
                lhsT=q_codes[:, t * P : (t + 1) * P].bitcast(FP8X4),
                lhsT_scale=q_scl[:, t * P : (t + 1) * P],
                rhs=k_codes[:].bitcast(FP8X4),
                rhs_scale=k_scl[:],
                start=True,
                stop=True,
            )
            st["z", u, t] = z

        def row_max(u, t):
            nc.vector.tensor_reduce(out=st["neg", u][:, t : t + 1], in_=st["z", u, t][:], axis=AX.X, op=ALU.max, negate=True)

        def row_bias(u, pair):
            cols = slice(2 * pair, 2 * pair + 2)
            nc.vector.tensor_scalar_mul(st["bias", u][:, cols], st["neg", u][:, cols], SCALE)

        def row_exp(u, t):
            nc.scalar.activation(
                out=st["e", u][:, t, :], in_=st["z", u, t][:], func=ACT.Exp, bias=st["bias", u][:, t : t + 1], scale=SCALE,
                accum_out=st["total", u][:, t : t + 1],
            )

        def inverse(u):
            if "S" in SC[u]:
                nc.vector.tensor_scalar_mul(st["inv", u][:], st["total", u][:], 1.0 / S)
                nc.vector.reciprocal(st["inv", u][:], st["inv", u][:])
            else:
                nc.vector.reciprocal(st["inv", u][:], st["total", u][:])

        def row_inverse(u, t):
            nc.vector.reciprocal(st["inv", u][:, t : t + 1], st["total", u][:, t : t + 1])

        left = {}

        def row_scale(u, t):
            b, h = UNITS[u]
            o, e, inv = st["o", u][:, t, :], st["e", u][:, t, :], st["inv", u][:, t : t + 1]
            if SC[u][t] == "S":
                nc.scalar.activation(out=o, in_=e, func=ACT.Copy, scale=inv)
            else:
                eng = nc.gpsimd if SC[u][t] == "G" else nc.vector
                eng.tensor_scalar(out=o, in0=e, scalar1=inv, scalar2=float(S), op0=ALU.mult, op1=ALU.mult)
            pair = t // 2
            left[u, pair] = left.get((u, pair), 0) + 1
            if left[u, pair] == 2:
                rows = slice(2 * pair, 2 * pair + 2)
                nc.sync.dma_start(out=out[b, h].rearrange("(p t) k -> p t k", t=PACK)[:, rows], in_=st["o", u][:, rows])

        def p_group(u, i):
            parts = len(PI[u])
            n = S // parts
            cols = slice(i * n, i * n + n)
            grouped = work.tile([P, n, PACK], BF16, name=f"p_grouped{parts}", bufs=3, align_bytes=64)
            st["pg", u, i] = grouped
            src = st["o", u][:, :, cols].rearrange("p t (k i) -> p k t i", i=4)
            dst = grouped[:].rearrange("p (k i) t -> p k t i", i=4)
            (nc.vector.tensor_copy if PI[u][i] == "V" else nc.scalar.copy)(out=dst, in_=src)

        def p_quant(u, i):
            b, h = UNITS[u]
            parts = len(PI[u])
            n = S // parts
            if ("pc", u) not in st:
                st["pc", u] = work.tile([P, S], U32, name="p_codes", bufs=3, align_bytes=64)
            codes = st["pc", u]
            first_row = 4 * (b * H + h)
            cols = slice(i * n, i * n + n)
            nc.vector.quantize_mx(
                out=codes[:, cols].bitcast(FP8X4), scales=p_scales[first_row:P, cols], in_=st["pg", u, i][:].rearrange("p k t -> p (k t)")
            )
            left["pq", u] = left.get(("pq", u), 0) + 1
            if left["pq", u] == parts:
                col = (b * H + h) * S
                nc.sync.dma_start(out=words32[:, col : col + S], in_=codes[:].bitcast(I32))
                left["all"] = left.get("all", 0) + 1
                if left["all"] == B * H:
                    for quad in range(4):
                        nc.sync.dma_start(
                            out=scales32[4 * quad : 4 * quad + 4, :].rearrange("r (u m) -> u r m", u=B * H),
                            in_=p_scales[32 * quad : 32 * quad + 16, :].bitcast(I32),
                        )

        def evacuate(n, u, c):
            if ("qg", u) not in st:
                open_unit(u)
            (q_out if n == "q" else k_out)(u, c)

        steps = {
            "lk": lk_turn, "xt": x_turn, "xc": x_copy, "xq": x_quant, "wt": w_turn, "wi": w_interleave, "wq": w_quant,
            "p": project, "ev": evacuate, "qz": lambda n, u: (q_quant if n == "q" else k_quant)(u),
            "z": score, "mx": row_max, "nb": row_bias, "ex": row_exp, "inv": inverse, "rc": row_inverse,
            "sc": row_scale, "pi": p_group, "pq": p_quant,
        }
        for name in ORDER:
            kind, *idx = name.split(".")
            steps[kind](*[a if a in ("q", "k") else int(a) for a in idx])
